import numpy as np
import ml_dtypes


def mxq(x, axis, fmt="e4m3"):
    dtype, down = {"e4m3": (ml_dtypes.float8_e4m3fn, 7), "e5m2": (ml_dtypes.float8_e5m2, 14)}[fmt]
    v = np.moveaxis(np.asarray(x, np.float32).astype(ml_dtypes.bfloat16).astype(np.float64), axis, -1)
    blocks = v.reshape(v.shape[:-1] + (-1, 32))
    amax = np.abs(blocks).max(-1, keepdims=True)
    byte = np.maximum(np.where(amax > 0, np.frexp(amax)[1] - 1 + 127, 0) - down, 1)
    scale = np.exp2(byte - 127.0)
    codes = (blocks / scale).astype(np.float32).astype(dtype).astype(np.float64)
    return np.moveaxis((codes * scale).reshape(v.shape), -1, axis)


WIDE = False


def mx_kscale(k):
    if not WIDE:
        return np.ones(k)
    levels = np.array([10, -10, 5, -5, 0])
    if k % 512:
        return np.exp2(np.random.permutation(np.resize(levels, k // 32))).repeat(32)
    a = np.empty((k // 512, 16))
    for p in range(k // 512):
        a[p, :8] = np.random.permutation(np.resize(levels, 8))
        for g in range(8):
            far = levels[np.abs(levels - a[p, g]) >= 10]
            a[p, g + 8] = far[np.random.randint(len(far))]
    return np.exp2(a.ravel()).repeat(32)


def f64(x):
    return np.asarray(x).astype(np.float64)


def striped(idx):
    return np.tile(idx.reshape(-1, 16).T, (8, 1)).astype(np.uint16)


def unstriped(offs):
    return offs[:16].T.reshape(-1).astype(np.int64)


def pack_weight(w):
    k, n = w.shape
    w = f64(np.asarray(w, np.float32).astype(ml_dtypes.bfloat16)).reshape(k // 32, 32, n)
    amax = np.abs(w).max(1)
    byte = np.clip(np.where(amax > 0, np.frexp(amax)[1] - 1 + 127 - 7, 1), 1, 254)
    scaled = (w * np.exp2(127.0 - byte)[:, None, :]).reshape(k, n).astype(np.float32)
    words = np.ascontiguousarray(scaled.reshape(k // 512, 128, 4, n).transpose(0, 1, 3, 2)).astype(ml_dtypes.float8_e4m3fn).view(np.uint8)
    return words, np.ascontiguousarray(byte.astype(np.uint8).reshape(k // 512, 16, n))


def unpack_weight(words, scales):
    g, p, n, _ = words.shape
    vals = np.ascontiguousarray(words).view(ml_dtypes.float8_e4m3fn).astype(np.float64) * np.repeat(np.exp2(scales.astype(np.float64) - 127.0), 8, axis=1)[..., None]
    return vals.transpose(0, 1, 3, 2).reshape(g * 512, n)


E2M1 = np.array([0.0, 0.5, 1.0, 1.5, 2.0, 3.0, 4.0, 6.0, -0.0, -0.5, -1.0, -1.5, -2.0, -3.0, -4.0, -6.0])


def pack_fp4(w):
    k, n = w.shape
    w = f64(np.asarray(w, np.float32).astype(ml_dtypes.bfloat16)).reshape(k // 32, 32, n)
    amax = np.abs(w).max(1)
    mant, ex = np.frexp(amax / 6.0)
    byte = np.clip(np.where(amax > 0, np.where(mant > 0.5, ex, ex - 1) + 127, 1), 1, 254)
    scaled = (w * np.exp2(127.0 - byte)[:, None, :]).reshape(k, n).astype(np.float32)
    c = np.ascontiguousarray(scaled.reshape(k // 512, 128, 4, n).transpose(0, 1, 3, 2)).astype(ml_dtypes.float4_e2m1fn).view(np.uint8) & 0xF
    words = (c[..., 0::2] | (c[..., 1::2] << 4)).reshape(k // 512, 128, 2 * n)
    return np.ascontiguousarray(words), np.ascontiguousarray(byte.astype(np.uint8).reshape(k // 512, 16, n))


def unpack_fp4(words, scales):
    g, _, n = scales.shape
    words = np.ascontiguousarray(words).reshape(g, 128, n, 2)
    nib = np.empty((g, 128, n, 4), np.uint8)
    nib[..., 0::2] = words & 0xF
    nib[..., 1::2] = words >> 4
    vals = E2M1[nib] * np.repeat(np.exp2(scales.astype(np.float64) - 127.0), 8, axis=1)[..., None]
    return vals.transpose(0, 1, 3, 2).reshape(g * 512, n)


def sigmoid(v):
    return 1.0 / (1.0 + np.exp(-np.maximum(v, -700.0)))


K, T, S, D, N, H = 512, 4096, 1024, 4, 256, 512


def setup_inputs():
    n = np.random.standard_normal
    s = mx_kscale(K)[:, None]
    u = mx_kscale(H)
    packed_xT = pack_weight(n((K, T)) * s)
    packed_w1 = pack_fp4(n((K, H)) / np.sqrt(K) / s)
    packed_w2 = pack_fp4(n((H, N)) / np.sqrt(H) / u[:, None])
    return {
        "x_words": packed_xT[0],
        "x_scales": packed_xT[1],
        "w1_words": packed_w1[0],
        "w1_scales": packed_w1[1],
        "xn": (np.random.uniform(0.3, 1.5, (H, S))).astype(np.float32),
        "unit": (np.random.uniform(0.6, 1.4, (H, 1)) * u[:, None]).astype(np.float32),
        "w2_words": packed_w2[0],
        "w2_scales": packed_w2[1],
        "offs": striped(np.random.permutation(T)[:S]),
        "pt": striped(np.random.permutation(S)),
    }


def reference(x_words, x_scales, w1_words, w1_scales, xn, unit, w2_words, w2_scales, offs, pt):
    xq = unpack_weight(x_words, x_scales)[:, unstriped(offs)]
    y = unpack_fp4(w1_words, w1_scales).T @ xq
    mag = np.abs(y)
    sal = mag * f64(xn)
    best = sal.reshape(len(sal), -1, D).max(axis=2)
    keepw = sigmoid(5.0 * (sal - (0.6 * np.repeat(best, D, axis=1))))
    drop = (-1.0 * keepw + 1.0) * y
    dropp = drop[:, unstriped(pt)]
    comp = keepw * y + 0.5 * dropp
    hid = f64(unit) * (comp * (np.repeat(best, D, axis=1) / (mag + 0.5)))
    return unpack_fp4(w2_words, w2_scales).T @ mxq(hid, 0, "e4m3")

@@ -1,0 +1,182 @@
+from contextlib import ExitStack
+
+import concourse.mybir as mybir
+
+K, T, S, D, N, H = 512, 4096, 1024, 4, 256, 512
+FLOPS = 2 * K * H * S + 2 * H * N * S
+
+F32 = mybir.dt.float32
+BF16 = mybir.dt.bfloat16
+I32 = mybir.dt.int32
+U32 = mybir.dt.uint32
+U16 = mybir.dt.uint16
+U8 = mybir.dt.uint8
+FP8X4 = mybir.dt.float8_e4m3fn_x4
+FP4X4 = mybir.dt.float4_e2m1fn_x4
+ALU = mybir.AluOpType
+ACT = mybir.ActivationFunctionType
+
+P = 128
+PACK = 4
+HALF = 512
+CHUNK = 256
+TINY = 1e-18
+
+
+def load_scale_rows(queue, plane, rows):
+    for r in range(4):
+        queue.dma_start(out=plane[r:P:32, :].bitcast(I32), in_=rows[r:16:4, :].bitcast(I32))
+
+
+def tile_picked_ylisax_scl_p_kernel(
+    tc, x_words, x_scales, w1_words, w1_scales, xn, unit, w2_words, w2_scales, offs, pt, out
+):
+    nc = tc.nc
+    halves = [slice(h * HALF, (h + 1) * HALF) for h in range(S // HALF)]
+    list_halves = [slice(h * HALF // 16, (h + 1) * HALF // 16) for h in range(S // HALF)]
+
+    with ExitStack() as ctx:
+        keep = ctx.enter_context(tc.tile_pool(name="keep", bufs=1))
+        ring = ctx.enter_context(tc.tile_pool(name="ring", bufs=2))
+        psum = ctx.enter_context(tc.psum_pool(name="psum", bufs=1))
+
+        offs_sb = keep.tile([P, S // 16], U16, name="offs_sb")
+        pt_sb = keep.tile([P, S // 16], U16, name="pt_sb")
+        xs_all = keep.tile([P, T], U8, name="xs_all")
+        xw_all = keep.tile([P, T], U32, name="xw_all")
+        w1w_raw = keep.tile([P, 2 * H], U8, name="w1w_raw")
+        w1s_raw = keep.tile([P, H], U8, name="w1s_raw")
+        w2w = keep.tile([P, 2 * N], U8, name="w2w", align_bytes=64)
+        w2s = keep.tile([P, N], U8, name="w2s", align_bytes=64)
+        unit_sb = keep.tile([P, PACK], F32, name="unit_sb")
+        xn_sb = [keep.tile([P, S], F32, name=f"xn{t}") for t in range(PACK)]
+
+        nc.vector.memset(xs_all[:].bitcast(I32), 0)
+        nc.gpsimd.memset(w1s_raw[:].bitcast(I32), 0)
+        nc.gpsimd.memset(w2s[:].bitcast(I32), 0)
+
+        xn_rows = xn.rearrange("(p t) s -> p t s", t=PACK)
+        nc.sync.dma_start(offs_sb[:], offs)
+        load_scale_rows(nc.sync, xs_all, x_scales[0])
+        nc.sync.dma_start(out=xw_all[:].bitcast(I32), in_=x_words[0].rearrange("p c r -> p (c r)").bitcast(I32))
+        nc.sync.dma_start(out=w1w_raw[:].bitcast(I32), in_=w1_words[0].bitcast(I32))
+        load_scale_rows(nc.sync, w1s_raw, w1_scales[0])
+        for t in range(PACK):
+            nc.sync.dma_start(out=xn_sb[t][:], in_=xn_rows[:, t, :])
+        nc.sync.dma_start(pt_sb[:], pt)
+        nc.sync.dma_start(out=unit_sb[:], in_=unit.rearrange("(p t) o -> p (t o)", t=PACK))
+        nc.sync.dma_start(out=w2w[:].bitcast(I32), in_=w2_words[0].bitcast(I32))
+        load_scale_rows(nc.sync, w2s, w2_scales[0])
+
+        xs = keep.tile([P, S], U8, name="xs", align_bytes=64)
+        nc.vector.tensor_copy(xs[:], xs_all[:].indirect(offs_sb[:]))
+        w1w = keep.tile([P, PACK, 2 * P], U8, name="w1w", align_bytes=64)
+        w1s = keep.tile([P, PACK, P], U8, name="w1s", align_bytes=64)
+        nc.vector.tensor_copy(
+            w1w[:].rearrange("p t (m b) -> p t m b", b=2),
+            w1w_raw[:].rearrange("p (m t b) -> p t m b", t=PACK, b=2),
+        )
+        nc.vector.tensor_copy(w1s[:], w1s_raw[:].rearrange("p (m t) -> p t m", t=PACK))
+
+        xw = [keep.tile([P, HALF], U32, name=f"xw{h}", align_bytes=64) for h in range(2)]
+        y = [[psum.tile([P, HALF], F32, name=f"bank{t}{h}") for h in range(2)] for t in range(PACK)]
+        for h in range(2):
+            nc.vector.tensor_copy(xw[h][:], xw_all[:].indirect(offs_sb[:, list_halves[h]]))
+        for t in range(PACK):
+            for h in range(2):
+                nc.tensor.matmul_mx(
+                    out=y[t][h][:],
+                    lhsT=w1w[:, t, :].bitcast(FP4X4),
+                    lhsT_scale=w1s[:, t, :],
+                    rhs=xw[h][:].bitcast(FP8X4),
+                    rhs_scale=xs[:, halves[h]],
+                    start=True,
+                    stop=True,
+                )
+
+        neg2unit = keep.tile([P, PACK], F32, name="neg2unit")
+        nc.vector.tensor_scalar(neg2unit[:], unit_sb[:], -2.0, None, ALU.mult)
+
+        mag = [keep.tile([P, S], F32, name=f"mag{t}") for t in range(PACK)]
+        lnm = [keep.tile([P, S], F32, name=f"lnm{t}") for t in range(PACK)]
+        best = [keep.tile([P, S // D], F32, name=f"best{t}") for t in range(PACK)]
+        margin = [keep.tile([P, S], F32, name=f"margin{t}") for t in range(PACK)]
+        for t in range(PACK):
+            for h in range(2):
+                nc.scalar.activation(mag[t][:, halves[h]], y[t][h][:], ACT.Abs)
+        for t in range(PACK):
+            nc.scalar.activation(lnm[t][:], mag[t][:], ACT.Ln, bias=TINY, scale=2.0)
+        for t in range(PACK):
+            sal = ring.tile([P, S], F32, name="sal")
+            nc.vector.tensor_tensor(sal[:], mag[t][:], xn_sb[t][:], ALU.mult)
+            groups = sal[:].rearrange("p (v d) -> p v d", d=D)
+            nc.vector.tensor_reduce(best[t][:], groups, mybir.AxisListType.X, ALU.max)
+            nc.vector.scalar_tensor_tensor(
+                margin[t][:].rearrange("p (v d) -> p v d", d=D),
+                best[t][:].unsqueeze(2).to_broadcast([P, S // D, D]),
+                -0.6,
+                groups,
+                ALU.mult,
+                ALU.add,
+            )
+
+        drop = [keep.tile([P, S], F32, name=f"drop{t}") for t in range(PACK)]
+        negkept = [keep.tile([P, S], F32, name=f"negkept{t}") for t in range(PACK)]
+        factor = keep.tile([P, PACK, S], F32, name="factor")
+        for t in range(PACK):
+            dropw = ring.tile([P, S], F32, name="dropw")
+            nc.scalar.activation(dropw[:], margin[t][:], ACT.Sigmoid, scale=-5.0)
+            for h in range(2):
+                nc.vector.scalar_tensor_tensor(
+                    drop[t][:, halves[h]], dropw[:, halves[h]], unit_sb[:, t : t + 1], y[t][h][:], ALU.mult, ALU.mult
+                )
+            for h in range(2):
+                nc.vector.scalar_tensor_tensor(
+                    negkept[t][:, halves[h]], dropw[:, halves[h]], -1.0, y[t][h][:], ALU.add, ALU.mult
+                )
+        for t in range(PACK):
+            halfrec = ring.tile([P, S], F32, name="halfrec")
+            nc.scalar.activation(halfrec[:], lnm[t][:], ACT.Sigmoid, scale=-1.0)
+            nc.vector.tensor_tensor(
+                factor[:, t, :].rearrange("p (v d) -> p v d", d=D),
+                halfrec[:].rearrange("p (v d) -> p v d", d=D),
+                best[t][:].unsqueeze(2).to_broadcast([P, S // D, D]),
+                ALU.mult,
+            )
+
+        out_rows = out.rearrange("(m p) s -> p m s", p=P)
+        for h in range(2):
+            comp = ring.tile([P, PACK, HALF], F32, name="comp")
+            for t in range(PACK):
+                partner = ring.tile([P, HALF], F32, name="partner", bufs=4)
+                nc.scalar.activation(partner[:], drop[t][:].indirect(pt_sb[:, list_halves[h]]), ACT.Copy)
+                nc.vector.scalar_tensor_tensor(
+                    comp[:, t, :], negkept[t][:, halves[h]], neg2unit[:, t : t + 1], partner[:], ALU.mult, ALU.add
+                )
+            for c in range(HALF // CHUNK):
+                local = slice(c * CHUNK, (c + 1) * CHUNK)
+                cols = slice(h * HALF + c * CHUNK, h * HALF + (c + 1) * CHUNK)
+                hid = ring.tile([P, CHUNK, PACK], BF16, name="hid", align_bytes=64)
+                nc.vector.tensor_tensor(
+                    hid[:].rearrange("p (c i) t -> p c t i", i=4),
+                    comp[:, :, local].rearrange("p t (c i) -> p c t i", i=4),
+                    factor[:, :, cols].rearrange("p t (c i) -> p c t i", i=4),
+                    ALU.mult,
+                )
+                hw = ring.tile([P, CHUNK], U32, name="hw", align_bytes=64)
+                hs = ring.tile([P, CHUNK], U8, name="hs", align_bytes=64)
+                nc.vector.quantize_mx(out=hw[:].bitcast(FP8X4), scales=hs[:], in_=hid[:].rearrange("p c t -> p (c t)"))
+                acc = psum.tile([P, HALF], F32, name=f"bank{c}{h}")
+                for m in range(N // P):
+                    nc.tensor.matmul_mx(
+                        out=acc[:, m * CHUNK : (m + 1) * CHUNK],
+                        lhsT=w2w[:, 2 * P * m : 2 * P * (m + 1)].bitcast(FP4X4),
+                        lhsT_scale=w2s[:, P * m : P * (m + 1)],
+                        rhs=hw[:].bitcast(FP8X4),
+                        rhs_scale=hs[:],
+                        start=True,
+                        stop=True,
+                    )
+                res = ring.tile([P, N // P, CHUNK], F32, name="res")
+                nc.scalar.copy(res[:].rearrange("p m c -> p (m c)"), acc[:])
+                nc.sync.dma_start(out=out_rows[:, :, cols], in_=res[:])

@@ -42,34 +42,28 @@ def tile_picked_ylisax_scl_p_kernel(
 
         offs_sb = keep.tile([P, S // 16], U16, name="offs_sb")
         pt_sb = keep.tile([P, S // 16], U16, name="pt_sb")
-        xs_all = keep.tile([P, T], U8, name="xs_all")
-        xw_all = keep.tile([P, T], U32, name="xw_all")
-        w1w_raw = keep.tile([P, 2 * H], U8, name="w1w_raw")
-        w1s_raw = keep.tile([P, H], U8, name="w1s_raw")
-        w2w = keep.tile([P, 2 * N], U8, name="w2w", align_bytes=64)
-        w2s = keep.tile([P, N], U8, name="w2s", align_bytes=64)
+        xs_all = keep.tile([P, T], U8, name="xs_all", tag="slot_b")
+        xw_all = keep.tile([P, T], U32, name="xw_all", tag="slot_c")
+        w1w_raw = keep.tile([P, 2 * H], U8, name="w1w_raw", tag="slot_a", align_bytes=64)
+        w1s_raw = keep.tile([P, H], U8, name="w1s_raw", tag="weight_scales", align_bytes=64)
         unit_sb = keep.tile([P, PACK], F32, name="unit_sb")
-        xn_sb = [keep.tile([P, S], F32, name=f"xn{t}") for t in range(PACK)]
 
         nc.vector.memset(xs_all[:].bitcast(I32), 0)
         nc.gpsimd.memset(w1s_raw[:].bitcast(I32), 0)
-        nc.gpsimd.memset(w2s[:].bitcast(I32), 0)
 
         xn_rows = xn.rearrange("(p t) s -> p t s", t=PACK)
         nc.sync.dma_start(offs_sb[:], offs)
-        load_scale_rows(nc.sync, xs_all, x_scales[0])
         nc.sync.dma_start(out=xw_all[:].bitcast(I32), in_=x_words[0].rearrange("p c r -> p (c r)").bitcast(I32))
-        nc.sync.dma_start(out=w1w_raw[:].bitcast(I32), in_=w1_words[0].bitcast(I32))
-        load_scale_rows(nc.sync, w1s_raw, w1_scales[0])
-        for t in range(PACK):
-            nc.sync.dma_start(out=xn_sb[t][:], in_=xn_rows[:, t, :])
+        nc.scalar.dma_start(out=w1w_raw[:].bitcast(I32), in_=w1_words[0].bitcast(I32))
+        load_scale_rows(nc.scalar, xs_all, x_scales[0])
+        load_scale_rows(nc.gpsimd, w1s_raw, w1_scales[0])
         nc.sync.dma_start(pt_sb[:], pt)
-        nc.sync.dma_start(out=unit_sb[:], in_=unit.rearrange("(p t) o -> p (t o)", t=PACK))
-        nc.sync.dma_start(out=w2w[:].bitcast(I32), in_=w2_words[0].bitcast(I32))
-        load_scale_rows(nc.sync, w2s, w2_scales[0])
+        nc.gpsimd.dma_start(out=unit_sb[:], in_=unit.rearrange("(p t) o -> p (t o)", t=PACK))
 
-        xs = keep.tile([P, S], U8, name="xs", align_bytes=64)
-        nc.vector.tensor_copy(xs[:], xs_all[:].indirect(offs_sb[:]))
+        warm = keep.tile([P, 2], F32, name="warm")
+        nc.vector.memset(warm[:, 0:1], 1.0)
+        nc.scalar.activation(warm[:, 1:2], warm[:, 0:1], ACT.Ln, bias=TINY, scale=2.0)
+
         w1w = keep.tile([P, PACK, 2 * P], U8, name="w1w", align_bytes=64)
         w1s = keep.tile([P, PACK, P], U8, name="w1s", align_bytes=64)
         nc.vector.tensor_copy(
@@ -78,9 +72,11 @@ def tile_picked_ylisax_scl_p_kernel(
         )
         nc.vector.tensor_copy(w1s[:], w1s_raw[:].rearrange("p (m t) -> p t m", t=PACK))
 
+        xs = [keep.tile([P, HALF], U8, name=f"xs{h}", align_bytes=64) for h in range(2)]
         xw = [keep.tile([P, HALF], U32, name=f"xw{h}", align_bytes=64) for h in range(2)]
         y = [[psum.tile([P, HALF], F32, name=f"bank{t}{h}") for h in range(2)] for t in range(PACK)]
         for h in range(2):
+            nc.vector.tensor_copy(xs[h][:], xs_all[:].indirect(offs_sb[:, list_halves[h]]))
             nc.vector.tensor_copy(xw[h][:], xw_all[:].indirect(offs_sb[:, list_halves[h]]))
         for t in range(PACK):
             for h in range(2):
@@ -89,10 +85,21 @@ def tile_picked_ylisax_scl_p_kernel(
                     lhsT=w1w[:, t, :].bitcast(FP4X4),
                     lhsT_scale=w1s[:, t, :],
                     rhs=xw[h][:].bitcast(FP8X4),
-                    rhs_scale=xs[:, halves[h]],
+                    rhs_scale=xs[h][:],
                     start=True,
                     stop=True,
                 )
+
+        xn0 = keep.tile([P, S], F32, name="xn0", tag="slot_a", align_bytes=64)
+        xn1 = keep.tile([P, S], F32, name="xn1", tag="slot_b")
+        xn23 = keep.tile([P, 2, S], F32, name="xn23", tag="slot_c")
+        nc.sync.dma_start(out=xn0[:], in_=xn_rows[:, 0, :])
+        nc.sync.dma_start(out=xn1[:], in_=xn_rows[:, 1, :])
+        nc.sync.dma_start(out=xn23[:], in_=xn_rows[:, 2:4, :])
+        xn_sb = [xn0[:], xn1[:], xn23[:, 0, :], xn23[:, 1, :]]
+        w2s = keep.tile([P, N], U8, name="w2s", tag="weight_scales", align_bytes=64)
+        nc.gpsimd.memset(w2s[:].bitcast(I32), 0)
+        load_scale_rows(nc.sync, w2s, w2_scales[0])
 
         neg2unit = keep.tile([P, PACK], F32, name="neg2unit")
         nc.vector.tensor_scalar(neg2unit[:], unit_sb[:], -2.0, None, ALU.mult)
@@ -106,19 +113,26 @@ def tile_picked_ylisax_scl_p_kernel(
                 nc.scalar.activation(mag[t][:, halves[h]], y[t][h][:], ACT.Abs)
         for t in range(PACK):
             nc.scalar.activation(lnm[t][:], mag[t][:], ACT.Ln, bias=TINY, scale=2.0)
-        for t in range(PACK):
-            sal = ring.tile([P, S], F32, name="sal")
-            nc.vector.tensor_tensor(sal[:], mag[t][:], xn_sb[t][:], ALU.mult)
-            groups = sal[:].rearrange("p (v d) -> p v d", d=D)
-            nc.vector.tensor_reduce(best[t][:], groups, mybir.AxisListType.X, ALU.max)
+        pieces = [(0, halves[0]), (0, halves[1])] + [(t, slice(0, S)) for t in range(1, PACK)]
+        for t, cols in pieces:
+            count = (cols.stop - cols.start) // D
+            best_piece = best[t][:, cols.start // D : cols.stop // D]
+            sal = ring.tile([P, count, D], F32, name="sal")
+            nc.vector.tensor_tensor(sal[:].rearrange("p v d -> p (v d)"), mag[t][:, cols], xn_sb[t][:, cols], ALU.mult)
+            pair = ring.tile([P, count, 2], F32, name="pair")
+            nc.vector.tensor_tensor(pair[:], sal[:, :, 0:2], sal[:, :, 2:4], ALU.max)
+            nc.vector.tensor_tensor(best_piece, pair[:, :, 0], pair[:, :, 1], ALU.max)
             nc.vector.scalar_tensor_tensor(
-                margin[t][:].rearrange("p (v d) -> p v d", d=D),
-                best[t][:].unsqueeze(2).to_broadcast([P, S // D, D]),
+                margin[t][:, cols].rearrange("p (v d) -> p v d", d=D),
+                best_piece.unsqueeze(2).to_broadcast([P, count, D]),
                 -0.6,
-                groups,
+                sal[:],
                 ALU.mult,
                 ALU.add,
             )
+
+        w2w = keep.tile([P, 2 * N], U8, name="w2w", tag="slot_a", align_bytes=64)
+        nc.sync.dma_start(out=w2w[:].bitcast(I32), in_=w2_words[0].bitcast(I32))
 
         drop = [keep.tile([P, S], F32, name=f"drop{t}") for t in range(PACK)]
         negkept = [keep.tile([P, S], F32, name=f"negkept{t}") for t in range(PACK)]
@@ -126,6 +140,8 @@ def tile_picked_ylisax_scl_p_kernel(
         for t in range(PACK):
             dropw = ring.tile([P, S], F32, name="dropw")
             nc.scalar.activation(dropw[:], margin[t][:], ACT.Sigmoid, scale=-5.0)
+            halfrec = ring.tile([P, S], F32, name="halfrec")
+            nc.scalar.activation(halfrec[:], lnm[t][:], ACT.Sigmoid, scale=-1.0)
             for h in range(2):
                 nc.vector.scalar_tensor_tensor(
                     drop[t][:, halves[h]], dropw[:, halves[h]], unit_sb[:, t : t + 1], y[t][h][:], ALU.mult, ALU.mult
@@ -134,10 +150,7 @@ def tile_picked_ylisax_scl_p_kernel(
                 nc.vector.scalar_tensor_tensor(
                     negkept[t][:, halves[h]], dropw[:, halves[h]], -1.0, y[t][h][:], ALU.add, ALU.mult
                 )
-        for t in range(PACK):
-            halfrec = ring.tile([P, S], F32, name="halfrec")
-            nc.scalar.activation(halfrec[:], lnm[t][:], ACT.Sigmoid, scale=-1.0)
-            nc.vector.tensor_tensor(
+            nc.gpsimd.tensor_tensor(
                 factor[:, t, :].rearrange("p (v d) -> p v d", d=D),
                 halfrec[:].rearrange("p (v d) -> p v d", d=D),
                 best[t][:].unsqueeze(2).to_broadcast([P, S // D, D]),
@@ -145,28 +158,28 @@ def tile_picked_ylisax_scl_p_kernel(
             )
 
         out_rows = out.rearrange("(m p) s -> p m s", p=P)
-        for h in range(2):
-            comp = ring.tile([P, PACK, HALF], F32, name="comp")
-            for t in range(PACK):
-                partner = ring.tile([P, HALF], F32, name="partner", bufs=4)
-                nc.scalar.activation(partner[:], drop[t][:].indirect(pt_sb[:, list_halves[h]]), ACT.Copy)
-                nc.vector.scalar_tensor_tensor(
-                    comp[:, t, :], negkept[t][:, halves[h]], neg2unit[:, t : t + 1], partner[:], ALU.mult, ALU.add
-                )
-            for c in range(HALF // CHUNK):
-                local = slice(c * CHUNK, (c + 1) * CHUNK)
-                cols = slice(h * HALF + c * CHUNK, h * HALF + (c + 1) * CHUNK)
+        for c in range(S // CHUNK):
+            if True:
+                cols = slice(c * CHUNK, (c + 1) * CHUNK)
+                comp = ring.tile([P, PACK, CHUNK], F32, name="comp")
+                for t in range(PACK):
+                    partner = ring.tile([P, CHUNK], F32, name="partner", bufs=8)
+                    entries = pt_sb[:, c * CHUNK // 16 : (c + 1) * CHUNK // 16]
+                    nc.scalar.activation(partner[:], drop[t][:].indirect(entries), ACT.Copy)
+                    nc.vector.scalar_tensor_tensor(
+                        comp[:, t, :], negkept[t][:, cols], neg2unit[:, t : t + 1], partner[:], ALU.mult, ALU.add
+                    )
                 hid = ring.tile([P, CHUNK, PACK], BF16, name="hid", align_bytes=64)
                 nc.vector.tensor_tensor(
                     hid[:].rearrange("p (c i) t -> p c t i", i=4),
-                    comp[:, :, local].rearrange("p t (c i) -> p c t i", i=4),
+                    comp[:].rearrange("p t (c i) -> p c t i", i=4),
                     factor[:, :, cols].rearrange("p t (c i) -> p c t i", i=4),
                     ALU.mult,
                 )
                 hw = ring.tile([P, CHUNK], U32, name="hw", align_bytes=64)
                 hs = ring.tile([P, CHUNK], U8, name="hs", align_bytes=64)
                 nc.vector.quantize_mx(out=hw[:].bitcast(FP8X4), scales=hs[:], in_=hid[:].rearrange("p c t -> p (c t)"))
-                acc = psum.tile([P, HALF], F32, name=f"bank{c}{h}")
+                acc = psum.tile([P, HALF], F32, name=f"bank{c // 2}{c % 2}")
                 for m in range(N // P):
                     nc.tensor.matmul_mx(
                         out=acc[:, m * CHUNK : (m + 1) * CHUNK],

@@ -21,10 +21,11 @@ PACK = 4
 HALF = 512
 CHUNK = 256
 TINY = 1e-18
+CLEAR_SPLIT = 576
 
 
-def load_scale_rows(queue, plane, rows):
-    for r in range(4):
+def load_scale_rows(queues, plane, rows):
+    for r, queue in enumerate(queues):
         queue.dma_start(out=plane[r:P:32, :].bitcast(I32), in_=rows[r:16:4, :].bitcast(I32))
 
 
@@ -48,17 +49,21 @@ def tile_picked_ylisax_scl_p_kernel(
         w1s_raw = keep.tile([P, H], U8, name="w1s_raw", tag="weight_scales", align_bytes=64)
         unit_sb = keep.tile([P, PACK], F32, name="unit_sb")
 
-        nc.vector.memset(xs_all[:].bitcast(I32), 0)
+        xs_zero = xs_all[:].bitcast(I32)
         nc.gpsimd.memset(w1s_raw[:].bitcast(I32), 0)
+        nc.gpsimd.memset(xs_zero[:, :CLEAR_SPLIT], 0)
+        nc.vector.memset(xs_zero[:, CLEAR_SPLIT:], 0)
 
         xn_rows = xn.rearrange("(p t) s -> p t s", t=PACK)
+        x_rows = x_words[0].rearrange("p c r -> p (c r)").bitcast(I32)
         nc.sync.dma_start(offs_sb[:], offs)
-        nc.sync.dma_start(out=xw_all[:].bitcast(I32), in_=x_words[0].rearrange("p c r -> p (c r)").bitcast(I32))
-        nc.scalar.dma_start(out=w1w_raw[:].bitcast(I32), in_=w1_words[0].bitcast(I32))
-        load_scale_rows(nc.scalar, xs_all, x_scales[0])
-        load_scale_rows(nc.gpsimd, w1s_raw, w1_scales[0])
+        nc.sync.dma_start(out=w1w_raw[:].bitcast(I32), in_=w1_words[0].bitcast(I32))
+        load_scale_rows([nc.sync] * 4, w1s_raw, w1_scales[0])
+        nc.sync.dma_start(out=xw_all[:].bitcast(I32)[:, : T // 2], in_=x_rows[:, : T // 2])
+        load_scale_rows([nc.sync] * 4, xs_all, x_scales[0])
+        nc.sync.dma_start(out=xw_all[:].bitcast(I32)[:, T // 2 :], in_=x_rows[:, T // 2 :])
         nc.sync.dma_start(pt_sb[:], pt)
-        nc.gpsimd.dma_start(out=unit_sb[:], in_=unit.rearrange("(p t) o -> p (t o)", t=PACK))
+        nc.sync.dma_start(out=unit_sb[:], in_=unit.rearrange("(p t) o -> p (t o)", t=PACK))
 
         warm = keep.tile([P, 2], F32, name="warm")
         nc.vector.memset(warm[:, 0:1], 1.0)
@@ -99,7 +104,7 @@ def tile_picked_ylisax_scl_p_kernel(
         xn_sb = [xn0[:], xn1[:], xn23[:, 0, :], xn23[:, 1, :]]
         w2s = keep.tile([P, N], U8, name="w2s", tag="weight_scales", align_bytes=64)
         nc.gpsimd.memset(w2s[:].bitcast(I32), 0)
-        load_scale_rows(nc.sync, w2s, w2_scales[0])
+        load_scale_rows([nc.sync] * 4, w2s, w2_scales[0])
 
         neg2unit = keep.tile([P, PACK], F32, name="neg2unit")
         nc.vector.tensor_scalar(neg2unit[:], unit_sb[:], -2.0, None, ALU.mult)
@@ -114,22 +119,38 @@ def tile_picked_ylisax_scl_p_kernel(
         for t in range(PACK):
             nc.scalar.activation(lnm[t][:], mag[t][:], ACT.Ln, bias=TINY, scale=2.0)
         pieces = [(0, halves[0]), (0, halves[1])] + [(t, slice(0, S)) for t in range(1, PACK)]
-        for t, cols in pieces:
+
+        def margin_steps(t, cols):
             count = (cols.stop - cols.start) // D
             best_piece = best[t][:, cols.start // D : cols.stop // D]
-            sal = ring.tile([P, count, D], F32, name="sal")
-            nc.vector.tensor_tensor(sal[:].rearrange("p v d -> p (v d)"), mag[t][:, cols], xn_sb[t][:, cols], ALU.mult)
+            sal = ring.tile([P, count, D], F32, name="sal", bufs=3)
             pair = ring.tile([P, count, 2], F32, name="pair")
-            nc.vector.tensor_tensor(pair[:], sal[:, :, 0:2], sal[:, :, 2:4], ALU.max)
-            nc.vector.tensor_tensor(best_piece, pair[:, :, 0], pair[:, :, 1], ALU.max)
-            nc.vector.scalar_tensor_tensor(
-                margin[t][:, cols].rearrange("p (v d) -> p v d", d=D),
-                best_piece.unsqueeze(2).to_broadcast([P, count, D]),
-                -0.6,
-                sal[:],
-                ALU.mult,
-                ALU.add,
-            )
+            return [
+                lambda: nc.vector.tensor_tensor(
+                    sal[:].rearrange("p v d -> p (v d)"), mag[t][:, cols], xn_sb[t][:, cols], ALU.mult
+                ),
+                lambda: nc.vector.tensor_tensor(pair[:], sal[:, :, 0:2], sal[:, :, 2:4], ALU.max),
+                lambda: nc.vector.tensor_tensor(best_piece, pair[:, :, 0], pair[:, :, 1], ALU.max),
+                lambda: nc.vector.scalar_tensor_tensor(
+                    margin[t][:, cols].rearrange("p (v d) -> p v d", d=D),
+                    best_piece.unsqueeze(2).to_broadcast([P, count, D]),
+                    -0.6,
+                    sal[:],
+                    ALU.mult,
+                    ALU.add,
+                ),
+            ]
+
+        behind = []
+        for t, cols in pieces:
+            steps = margin_steps(t, cols)
+            for i in range(2):
+                steps[i]()
+                if behind:
+                    behind[i]()
+            behind = steps[2:]
+        for step in behind:
+            step()
 
         w2w = keep.tile([P, 2 * N], U8, name="w2w", tag="slot_a", align_bytes=64)
         nc.sync.dma_start(out=w2w[:].bitcast(I32), in_=w2_words[0].bitcast(I32))
@@ -158,38 +179,46 @@ def tile_picked_ylisax_scl_p_kernel(
             )
 
         out_rows = out.rearrange("(m p) s -> p m s", p=P)
-        for c in range(S // CHUNK):
-            if True:
-                cols = slice(c * CHUNK, (c + 1) * CHUNK)
-                comp = ring.tile([P, PACK, CHUNK], F32, name="comp")
-                for t in range(PACK):
-                    partner = ring.tile([P, CHUNK], F32, name="partner", bufs=8)
-                    entries = pt_sb[:, c * CHUNK // 16 : (c + 1) * CHUNK // 16]
-                    nc.scalar.activation(partner[:], drop[t][:].indirect(entries), ACT.Copy)
-                    nc.vector.scalar_tensor_tensor(
-                        comp[:, t, :], negkept[t][:, cols], neg2unit[:, t : t + 1], partner[:], ALU.mult, ALU.add
-                    )
-                hid = ring.tile([P, CHUNK, PACK], BF16, name="hid", align_bytes=64)
-                nc.vector.tensor_tensor(
-                    hid[:].rearrange("p (c i) t -> p c t i", i=4),
-                    comp[:].rearrange("p t (c i) -> p c t i", i=4),
-                    factor[:, :, cols].rearrange("p t (c i) -> p c t i", i=4),
-                    ALU.mult,
+
+        def second_product(c, hid):
+            cols = slice(c * CHUNK, (c + 1) * CHUNK)
+            hw = ring.tile([P, CHUNK], U32, name="hw", align_bytes=64)
+            hs = ring.tile([P, CHUNK], U8, name="hs", align_bytes=64)
+            nc.vector.quantize_mx(out=hw[:].bitcast(FP8X4), scales=hs[:], in_=hid[:].rearrange("p c t -> p (c t)"))
+            acc = psum.tile([P, HALF], F32, name=f"bank{c // 2}{c % 2}")
+            for m in range(N // P):
+                nc.tensor.matmul_mx(
+                    out=acc[:, m * CHUNK : (m + 1) * CHUNK],
+                    lhsT=w2w[:, 2 * P * m : 2 * P * (m + 1)].bitcast(FP4X4),
+                    lhsT_scale=w2s[:, P * m : P * (m + 1)],
+                    rhs=hw[:].bitcast(FP8X4),
+                    rhs_scale=hs[:],
+                    start=True,
+                    stop=True,
                 )
-                hw = ring.tile([P, CHUNK], U32, name="hw", align_bytes=64)
-                hs = ring.tile([P, CHUNK], U8, name="hs", align_bytes=64)
-                nc.vector.quantize_mx(out=hw[:].bitcast(FP8X4), scales=hs[:], in_=hid[:].rearrange("p c t -> p (c t)"))
-                acc = psum.tile([P, HALF], F32, name=f"bank{c // 2}{c % 2}")
-                for m in range(N // P):
-                    nc.tensor.matmul_mx(
-                        out=acc[:, m * CHUNK : (m + 1) * CHUNK],
-                        lhsT=w2w[:, 2 * P * m : 2 * P * (m + 1)].bitcast(FP4X4),
-                        lhsT_scale=w2s[:, P * m : P * (m + 1)],
-                        rhs=hw[:].bitcast(FP8X4),
-                        rhs_scale=hs[:],
-                        start=True,
-                        stop=True,
-                    )
-                res = ring.tile([P, N // P, CHUNK], F32, name="res")
-                nc.scalar.copy(res[:].rearrange("p m c -> p (m c)"), acc[:])
-                nc.sync.dma_start(out=out_rows[:, :, cols], in_=res[:])
+            res = ring.tile([P, N // P, CHUNK], F32, name="res")
+            nc.scalar.copy(res[:].rearrange("p m c -> p (m c)"), acc[:])
+            nc.sync.dma_start(out=out_rows[:, :, cols], in_=res[:])
+
+        waiting = None
+        for c in range(S // CHUNK):
+            cols = slice(c * CHUNK, (c + 1) * CHUNK)
+            comp = ring.tile([P, PACK, CHUNK], F32, name="comp")
+            for t in range(PACK):
+                partner = ring.tile([P, CHUNK], F32, name="partner", bufs=8)
+                entries = pt_sb[:, c * CHUNK // 16 : (c + 1) * CHUNK // 16]
+                nc.scalar.activation(partner[:], drop[t][:].indirect(entries), ACT.Copy)
+                nc.vector.scalar_tensor_tensor(
+                    comp[:, t, :], negkept[t][:, cols], neg2unit[:, t : t + 1], partner[:], ALU.mult, ALU.add
+                )
+                if t == 0 and waiting is not None:
+                    second_product(c - 1, waiting)
+            hid = ring.tile([P, CHUNK, PACK], BF16, name="hid", align_bytes=64)
+            nc.vector.tensor_tensor(
+                hid[:].rearrange("p (c i) t -> p c t i", i=4),
+                comp[:].rearrange("p t (c i) -> p c t i", i=4),
+                factor[:, :, cols].rearrange("p t (c i) -> p c t i", i=4),
+                ALU.mult,
+            )
+            waiting = hid
+        second_product(S // CHUNK - 1, waiting)

@@ -123,7 +123,10 @@ def tile_picked_ylisax_scl_p_kernel(
         def margin_steps(t, cols):
             count = (cols.stop - cols.start) // D
             best_piece = best[t][:, cols.start // D : cols.stop // D]
-            sal = ring.tile([P, count, D], F32, name="sal", bufs=3)
+            if t == PACK - 1:
+                sal = keep.tile([P, count, D], F32, name="sal_last", tag="slot_d")
+            else:
+                sal = ring.tile([P, count, D], F32, name="sal", bufs=3)
             pair = ring.tile([P, count, 2], F32, name="pair")
             return [
                 lambda: nc.vector.tensor_tensor(
@@ -157,11 +160,21 @@ def tile_picked_ylisax_scl_p_kernel(
 
         drop = [keep.tile([P, S], F32, name=f"drop{t}") for t in range(PACK)]
         negkept = [keep.tile([P, S], F32, name=f"negkept{t}") for t in range(PACK)]
-        factor = keep.tile([P, PACK, S], F32, name="factor")
+        factor = keep.tile([P, PACK, S], F32, name="factor", tag="slot_d")
+
+        def make_factor(engine, t, halfrec, cols):
+            count = (cols.stop - cols.start) // D
+            engine.tensor_tensor(
+                factor[:, t, cols].rearrange("p (v d) -> p v d", d=D),
+                halfrec[:, cols].rearrange("p (v d) -> p v d", d=D),
+                best[t][:, cols.start // D : cols.stop // D].unsqueeze(2).to_broadcast([P, count, D]),
+                ALU.mult,
+            )
+
         for t in range(PACK):
-            dropw = ring.tile([P, S], F32, name="dropw")
+            dropw = ring.tile([P, S], F32, name="dropw", bufs=4)
             nc.scalar.activation(dropw[:], margin[t][:], ACT.Sigmoid, scale=-5.0)
-            halfrec = ring.tile([P, S], F32, name="halfrec")
+            halfrec = ring.tile([P, S], F32, name="halfrec", bufs=4)
             nc.scalar.activation(halfrec[:], lnm[t][:], ACT.Sigmoid, scale=-1.0)
             for h in range(2):
                 nc.vector.scalar_tensor_tensor(
@@ -171,12 +184,7 @@ def tile_picked_ylisax_scl_p_kernel(
                 nc.vector.scalar_tensor_tensor(
                     negkept[t][:, halves[h]], dropw[:, halves[h]], -1.0, y[t][h][:], ALU.add, ALU.mult
                 )
-            nc.gpsimd.tensor_tensor(
-                factor[:, t, :].rearrange("p (v d) -> p v d", d=D),
-                halfrec[:].rearrange("p (v d) -> p v d", d=D),
-                best[t][:].unsqueeze(2).to_broadcast([P, S // D, D]),
-                ALU.mult,
-            )
+            make_factor(nc.gpsimd, t, halfrec, slice(0, S if t < PACK - 1 else S - CHUNK))
 
         out_rows = out.rearrange("(m p) s -> p m s", p=P)
 
@@ -185,10 +193,12 @@ def tile_picked_ylisax_scl_p_kernel(
             hw = ring.tile([P, CHUNK], U32, name="hw", align_bytes=64)
             hs = ring.tile([P, CHUNK], U8, name="hs", align_bytes=64)
             nc.vector.quantize_mx(out=hw[:].bitcast(FP8X4), scales=hs[:], in_=hid[:].rearrange("p c t -> p (c t)"))
-            acc = psum.tile([P, HALF], F32, name=f"bank{c // 2}{c % 2}")
+            last = c == S // CHUNK - 1
+            acc = [psum.tile([P, HALF], F32, name=f"bank{c}{m}") for m in range(N // P if last else 1)]
+            res = ring.tile([P, N // P, CHUNK], F32, name="res")
             for m in range(N // P):
                 nc.tensor.matmul_mx(
-                    out=acc[:, m * CHUNK : (m + 1) * CHUNK],
+                    out=acc[m][:, :CHUNK] if last else acc[0][:, m * CHUNK : (m + 1) * CHUNK],
                     lhsT=w2w[:, 2 * P * m : 2 * P * (m + 1)].bitcast(FP4X4),
                     lhsT_scale=w2s[:, P * m : P * (m + 1)],
                     rhs=hw[:].bitcast(FP8X4),
@@ -196,9 +206,14 @@ def tile_picked_ylisax_scl_p_kernel(
                     start=True,
                     stop=True,
                 )
-            res = ring.tile([P, N // P, CHUNK], F32, name="res")
-            nc.scalar.copy(res[:].rearrange("p m c -> p (m c)"), acc[:])
-            nc.sync.dma_start(out=out_rows[:, :, cols], in_=res[:])
+            if last:
+                nc.scalar.copy(res[:, 0, :], acc[0][:, :CHUNK])
+                nc.scalar.dma_start(out=out_rows[:, 0, cols], in_=res[:, 0, :])
+                nc.vector.tensor_copy(res[:, 1, :], acc[1][:, :CHUNK])
+                nc.sync.dma_start(out=out_rows[:, 1, cols], in_=res[:, 1, :])
+            else:
+                nc.scalar.copy(res[:].rearrange("p m c -> p (m c)"), acc[0][:])
+                nc.sync.dma_start(out=out_rows[:, :, cols], in_=res[:])
 
         waiting = None
         for c in range(S // CHUNK):
@@ -213,6 +228,8 @@ def tile_picked_ylisax_scl_p_kernel(
                 )
                 if t == 0 and waiting is not None:
                     second_product(c - 1, waiting)
+            if c == S // CHUNK - 1:
+                make_factor(nc.vector, PACK - 1, halfrec, cols)
             hid = ring.tile([P, CHUNK, PACK], BF16, name="hid", align_bytes=64)
             nc.vector.tensor_tensor(
                 hid[:].rearrange("p (c i) t -> p c t i", i=4),

@@ -127,7 +127,10 @@ def tile_picked_ylisax_scl_p_kernel(
                 sal = keep.tile([P, count, D], F32, name="sal_last", tag="slot_d")
             else:
                 sal = ring.tile([P, count, D], F32, name="sal", bufs=3)
-            pair = ring.tile([P, count, 2], F32, name="pair")
+            if t == PACK - 1:
+                pair = keep.tile([P, count, 2], F32, name="pair_last", tag="drop0")
+            else:
+                pair = ring.tile([P, count, 2], F32, name="pair")
             return [
                 lambda: nc.vector.tensor_tensor(
                     sal[:].rearrange("p v d -> p (v d)"), mag[t][:, cols], xn_sb[t][:, cols], ALU.mult
@@ -159,7 +162,7 @@ def tile_picked_ylisax_scl_p_kernel(
         nc.sync.dma_start(out=w2w[:].bitcast(I32), in_=w2_words[0].bitcast(I32))
 
         drop = [keep.tile([P, S], F32, name=f"drop{t}") for t in range(PACK)]
-        negkept = [keep.tile([P, S], F32, name=f"negkept{t}") for t in range(PACK)]
+        negkept = [keep.tile([P, S], F32, name=f"negkept{t}", tag=f"mag{PACK - 1 - t}") for t in range(PACK)]
         factor = keep.tile([P, PACK, S], F32, name="factor", tag="slot_d")
 
         def make_factor(engine, t, halfrec, cols):
@@ -184,7 +187,8 @@ def tile_picked_ylisax_scl_p_kernel(
                 nc.vector.scalar_tensor_tensor(
                     negkept[t][:, halves[h]], dropw[:, halves[h]], -1.0, y[t][h][:], ALU.add, ALU.mult
                 )
-            make_factor(nc.gpsimd, t, halfrec, slice(0, S if t < PACK - 1 else S - CHUNK))
+            if t < PACK - 1:
+                make_factor(nc.gpsimd, t, halfrec, slice(0, S))
 
         out_rows = out.rearrange("(m p) s -> p m s", p=P)
 
@@ -226,10 +230,10 @@ def tile_picked_ylisax_scl_p_kernel(
                 nc.vector.scalar_tensor_tensor(
                     comp[:, t, :], negkept[t][:, cols], neg2unit[:, t : t + 1], partner[:], ALU.mult, ALU.add
                 )
-                if t == 0 and waiting is not None:
-                    second_product(c - 1, waiting)
-            if c == S // CHUNK - 1:
-                make_factor(nc.vector, PACK - 1, halfrec, cols)
+                if t == PACK - 2:
+                    make_factor(nc.vector, PACK - 1, halfrec, cols)
+            if waiting is not None:
+                second_product(c - 1, waiting)
             hid = ring.tile([P, CHUNK, PACK], BF16, name="hid", align_bytes=64)
             nc.vector.tensor_tensor(
                 hid[:].rearrange("p (c i) t -> p c t i", i=4),

from contextlib import ExitStack

import concourse.mybir as mybir

K, T, S, D, N, H = 512, 4096, 1024, 4, 256, 512
FLOPS = 2 * K * H * S + 2 * H * N * S

F32 = mybir.dt.float32
BF16 = mybir.dt.bfloat16
I32 = mybir.dt.int32
U32 = mybir.dt.uint32
U16 = mybir.dt.uint16
U8 = mybir.dt.uint8
FP8X4 = mybir.dt.float8_e4m3fn_x4
FP4X4 = mybir.dt.float4_e2m1fn_x4
ALU = mybir.AluOpType
ACT = mybir.ActivationFunctionType

P = 128
PACK = 4
HALF = 512
CHUNK = 256
TINY = 1e-18
CLEAR_SPLIT = 576


def load_scale_rows(queues, plane, rows):
    for r, queue in enumerate(queues):
        queue.dma_start(out=plane[r:P:32, :].bitcast(I32), in_=rows[r:16:4, :].bitcast(I32))


def tile_picked_ylisax_scl_p_kernel(
    tc, x_words, x_scales, w1_words, w1_scales, xn, unit, w2_words, w2_scales, offs, pt, out
):
    nc = tc.nc
    halves = [slice(h * HALF, (h + 1) * HALF) for h in range(S // HALF)]
    list_halves = [slice(h * HALF // 16, (h + 1) * HALF // 16) for h in range(S // HALF)]

    with ExitStack() as ctx:
        keep = ctx.enter_context(tc.tile_pool(name="keep", bufs=1))
        ring = ctx.enter_context(tc.tile_pool(name="ring", bufs=2))
        psum = ctx.enter_context(tc.psum_pool(name="psum", bufs=1))

        offs_sb = keep.tile([P, S // 16], U16, name="offs_sb")
        pt_sb = keep.tile([P, S // 16], U16, name="pt_sb")
        xs_all = keep.tile([P, T], U8, name="xs_all", tag="slot_b")
        xw_all = keep.tile([P, T], U32, name="xw_all", tag="slot_c")
        w1w_raw = keep.tile([P, 2 * H], U8, name="w1w_raw", tag="slot_a", align_bytes=64)
        w1s_raw = keep.tile([P, H], U8, name="w1s_raw", tag="weight_scales", align_bytes=64)
        unit_sb = keep.tile([P, PACK], F32, name="unit_sb")

        xs_zero = xs_all[:].bitcast(I32)
        nc.gpsimd.memset(w1s_raw[:].bitcast(I32), 0)
        nc.gpsimd.memset(xs_zero[:, :CLEAR_SPLIT], 0)
        nc.vector.memset(xs_zero[:, CLEAR_SPLIT:], 0)

        xn_rows = xn.rearrange("(p t) s -> p t s", t=PACK)
        x_rows = x_words[0].rearrange("p c r -> p (c r)").bitcast(I32)
        nc.sync.dma_start(offs_sb[:], offs)
        nc.sync.dma_start(out=w1w_raw[:].bitcast(I32), in_=w1_words[0].bitcast(I32))
        load_scale_rows([nc.sync] * 4, w1s_raw, w1_scales[0])
        nc.sync.dma_start(out=xw_all[:].bitcast(I32)[:, : T // 2], in_=x_rows[:, : T // 2])
        load_scale_rows([nc.sync] * 4, xs_all, x_scales[0])
        nc.sync.dma_start(out=xw_all[:].bitcast(I32)[:, T // 2 :], in_=x_rows[:, T // 2 :])
        nc.sync.dma_start(pt_sb[:], pt)
        nc.sync.dma_start(out=unit_sb[:], in_=unit.rearrange("(p t) o -> p (t o)", t=PACK))

        warm = keep.tile([P, 2], F32, name="warm")
        nc.vector.memset(warm[:, 0:1], 1.0)
        nc.scalar.activation(warm[:, 1:2], warm[:, 0:1], ACT.Ln, bias=TINY, scale=2.0)

        w1w = keep.tile([P, PACK, 2 * P], U8, name="w1w", align_bytes=64)
        w1s = keep.tile([P, PACK, P], U8, name="w1s", align_bytes=64)
        nc.vector.tensor_copy(
            w1w[:].rearrange("p t (m b) -> p t m b", b=2),
            w1w_raw[:].rearrange("p (m t b) -> p t m b", t=PACK, b=2),
        )
        nc.vector.tensor_copy(w1s[:], w1s_raw[:].rearrange("p (m t) -> p t m", t=PACK))

        xs = [keep.tile([P, HALF], U8, name=f"xs{h}", align_bytes=64) for h in range(2)]
        xw = [keep.tile([P, HALF], U32, name=f"xw{h}", align_bytes=64) for h in range(2)]
        y = [[psum.tile([P, HALF], F32, name=f"bank{t}{h}") for h in range(2)] for t in range(PACK)]
        for h in range(2):
            nc.vector.tensor_copy(xs[h][:], xs_all[:].indirect(offs_sb[:, list_halves[h]]))
            nc.vector.tensor_copy(xw[h][:], xw_all[:].indirect(offs_sb[:, list_halves[h]]))
        for t in range(PACK):
            for h in range(2):
                nc.tensor.matmul_mx(
                    out=y[t][h][:],
                    lhsT=w1w[:, t, :].bitcast(FP4X4),
                    lhsT_scale=w1s[:, t, :],
                    rhs=xw[h][:].bitcast(FP8X4),
                    rhs_scale=xs[h][:],
                    start=True,
                    stop=True,
                )

        xn0 = keep.tile([P, S], F32, name="xn0", tag="slot_a", align_bytes=64)
        xn1 = keep.tile([P, S], F32, name="xn1", tag="slot_b")
        xn23 = keep.tile([P, 2, S], F32, name="xn23", tag="slot_c")
        nc.sync.dma_start(out=xn0[:], in_=xn_rows[:, 0, :])
        nc.sync.dma_start(out=xn1[:], in_=xn_rows[:, 1, :])
        nc.sync.dma_start(out=xn23[:], in_=xn_rows[:, 2:4, :])
        xn_sb = [xn0[:], xn1[:], xn23[:, 0, :], xn23[:, 1, :]]
        w2s = keep.tile([P, N], U8, name="w2s", tag="weight_scales", align_bytes=64)
        nc.gpsimd.memset(w2s[:].bitcast(I32), 0)
        load_scale_rows([nc.sync] * 4, w2s, w2_scales[0])

        neg2unit = keep.tile([P, PACK], F32, name="neg2unit")
        nc.vector.tensor_scalar(neg2unit[:], unit_sb[:], -2.0, None, ALU.mult)

        mag = [keep.tile([P, S], F32, name=f"mag{t}") for t in range(PACK)]
        lnm = [keep.tile([P, S], F32, name=f"lnm{t}") for t in range(PACK)]
        best = [keep.tile([P, S // D], F32, name=f"best{t}") for t in range(PACK)]
        margin = [keep.tile([P, S], F32, name=f"margin{t}") for t in range(PACK)]
        for t in range(PACK):
            for h in range(2):
                nc.scalar.activation(mag[t][:, halves[h]], y[t][h][:], ACT.Abs)
        for t in range(PACK):
            nc.scalar.activation(lnm[t][:], mag[t][:], ACT.Ln, bias=TINY, scale=2.0)
        pieces = [(0, halves[0]), (0, halves[1])] + [(t, slice(0, S)) for t in range(1, PACK)]

        def margin_steps(t, cols):
            count = (cols.stop - cols.start) // D
            best_piece = best[t][:, cols.start // D : cols.stop // D]
            if t == PACK - 1:
                sal = keep.tile([P, count, D], F32, name="sal_last", tag="slot_d")
            else:
                sal = ring.tile([P, count, D], F32, name="sal", bufs=3)
            if t == PACK - 1:
                pair = keep.tile([P, count, 2], F32, name="pair_last", tag="drop0")
            else:
                pair = ring.tile([P, count, 2], F32, name="pair")
            return [
                lambda: nc.vector.tensor_tensor(
                    sal[:].rearrange("p v d -> p (v d)"), mag[t][:, cols], xn_sb[t][:, cols], ALU.mult
                ),
                lambda: nc.vector.tensor_tensor(pair[:], sal[:, :, 0:2], sal[:, :, 2:4], ALU.max),
                lambda: nc.vector.tensor_tensor(best_piece, pair[:, :, 0], pair[:, :, 1], ALU.max),
                lambda: nc.vector.scalar_tensor_tensor(
                    margin[t][:, cols].rearrange("p (v d) -> p v d", d=D),
                    best_piece.unsqueeze(2).to_broadcast([P, count, D]),
                    -0.6,
                    sal[:],
                    ALU.mult,
                    ALU.add,
                ),
            ]

        behind = []
        for t, cols in pieces:
            steps = margin_steps(t, cols)
            for i in range(2):
                steps[i]()
                if behind:
                    behind[i]()
            behind = steps[2:]
        for step in behind:
            step()

        w2w = keep.tile([P, 2 * N], U8, name="w2w", tag="slot_a", align_bytes=64)
        nc.sync.dma_start(out=w2w[:].bitcast(I32), in_=w2_words[0].bitcast(I32))

        drop = [keep.tile([P, S], F32, name=f"drop{t}") for t in range(PACK)]
        negkept = [keep.tile([P, S], F32, name=f"negkept{t}", tag=f"mag{PACK - 1 - t}") for t in range(PACK)]
        factor = keep.tile([P, PACK, S], F32, name="factor", tag="slot_d")

        def make_factor(engine, t, halfrec, cols):
            count = (cols.stop - cols.start) // D
            engine.tensor_tensor(
                factor[:, t, cols].rearrange("p (v d) -> p v d", d=D),
                halfrec[:, cols].rearrange("p (v d) -> p v d", d=D),
                best[t][:, cols.start // D : cols.stop // D].unsqueeze(2).to_broadcast([P, count, D]),
                ALU.mult,
            )

        for t in range(PACK):
            dropw = ring.tile([P, S], F32, name="dropw", bufs=4)
            nc.scalar.activation(dropw[:], margin[t][:], ACT.Sigmoid, scale=-5.0)
            halfrec = ring.tile([P, S], F32, name="halfrec", bufs=4)
            nc.scalar.activation(halfrec[:], lnm[t][:], ACT.Sigmoid, scale=-1.0)
            for h in range(2):
                nc.vector.scalar_tensor_tensor(
                    drop[t][:, halves[h]], dropw[:, halves[h]], unit_sb[:, t : t + 1], y[t][h][:], ALU.mult, ALU.mult
                )
            for h in range(2):
                nc.vector.scalar_tensor_tensor(
                    negkept[t][:, halves[h]], dropw[:, halves[h]], -1.0, y[t][h][:], ALU.add, ALU.mult
                )
            if t < PACK - 1:
                make_factor(nc.gpsimd, t, halfrec, slice(0, S))

        out_rows = out.rearrange("(m p) s -> p m s", p=P)

        def second_product(c, hid):
            cols = slice(c * CHUNK, (c + 1) * CHUNK)
            hw = ring.tile([P, CHUNK], U32, name="hw", align_bytes=64)
            hs = ring.tile([P, CHUNK], U8, name="hs", align_bytes=64)
            nc.vector.quantize_mx(out=hw[:].bitcast(FP8X4), scales=hs[:], in_=hid[:].rearrange("p c t -> p (c t)"))
            last = c == S // CHUNK - 1
            acc = [psum.tile([P, HALF], F32, name=f"bank{c}{m}") for m in range(N // P if last else 1)]
            res = ring.tile([P, N // P, CHUNK], F32, name="res")
            for m in range(N // P):
                nc.tensor.matmul_mx(
                    out=acc[m][:, :CHUNK] if last else acc[0][:, m * CHUNK : (m + 1) * CHUNK],
                    lhsT=w2w[:, 2 * P * m : 2 * P * (m + 1)].bitcast(FP4X4),
                    lhsT_scale=w2s[:, P * m : P * (m + 1)],
                    rhs=hw[:].bitcast(FP8X4),
                    rhs_scale=hs[:],
                    start=True,
                    stop=True,
                )
            if last:
                nc.scalar.copy(res[:, 0, :], acc[0][:, :CHUNK])
                nc.scalar.dma_start(out=out_rows[:, 0, cols], in_=res[:, 0, :])
                nc.vector.tensor_copy(res[:, 1, :], acc[1][:, :CHUNK])
                nc.sync.dma_start(out=out_rows[:, 1, cols], in_=res[:, 1, :])
            else:
                nc.scalar.copy(res[:].rearrange("p m c -> p (m c)"), acc[0][:])
                nc.sync.dma_start(out=out_rows[:, :, cols], in_=res[:])

        waiting = None
        for c in range(S // CHUNK):
            cols = slice(c * CHUNK, (c + 1) * CHUNK)
            comp = ring.tile([P, PACK, CHUNK], F32, name="comp")
            for t in range(PACK):
                partner = ring.tile([P, CHUNK], F32, name="partner", bufs=8)
                entries = pt_sb[:, c * CHUNK // 16 : (c + 1) * CHUNK // 16]
                nc.scalar.activation(partner[:], drop[t][:].indirect(entries), ACT.Copy)
                nc.vector.scalar_tensor_tensor(
                    comp[:, t, :], negkept[t][:, cols], neg2unit[:, t : t + 1], partner[:], ALU.mult, ALU.add
                )
                if t == PACK - 2:
                    make_factor(nc.vector, PACK - 1, halfrec, cols)
            if waiting is not None:
                second_product(c - 1, waiting)
            hid = ring.tile([P, CHUNK, PACK], BF16, name="hid", align_bytes=64)
            nc.vector.tensor_tensor(
                hid[:].rearrange("p (c i) t -> p c t i", i=4),
                comp[:].rearrange("p t (c i) -> p c t i", i=4),
                factor[:, :, cols].rearrange("p t (c i) -> p c t i", i=4),
                ALU.mult,
            )
            waiting = hid
        second_product(S // CHUNK - 1, waiting)
